import numpy as np
CORES = [0,1,2,3]
N = 4
ROOT = 1
WIDTHS = [3,40,9,20]
XW = 40
def setup_inputs(rng):
    return {"x": rng.standard_normal((N, 128, XW), dtype=np.float32)}
def reference(x):
    g = np.concatenate([x[r][:, :WIDTHS[r]] for r in range(N)], axis=1)
    y = np.full((N, 128, g.shape[1]), np.nan, x.dtype)
    y[ROOT] = g
    return {"y": y}

SCRATCH = {
    "land": ("sbuf", [128, 72], "float32"),
}
SEMAPHORES = ["loaded", "read", "arrived", "stored"]

ENGINES = 16


def rank_program(g, core, T, topo):
    rank = T.rank_of(core)
    if rank is None:
        return

    widths = T.tables["WIDTHS"]
    root = T.root if T.root is not None else 1
    root_core = T.cores[root]
    off = sum(widths[:rank])
    w = widths[rank]
    mine = T.land[:, off:off + w]

    g.dma_start(mine, T.x[:, 0:w]).then_inc(T.sem.loaded, ENGINES)
    g.wait_ge(T.sem.loaded, ENGINES)

    if rank != root:
        rid, pid, sengine = topo.addr(root_core)
        g.remote_dma(mine, mine, T.sem.arrived, T.sem.read, pid, rid, topo.mask(core, root_core))
        g.wait_ge(T.sem.read, ENGINES)
        return

    g.wait_ge(T.sem.arrived, ENGINES * (len(T.cores) - 1))
    g.dma_start(T.y[:, :], T.land[:, :]).then_inc(T.sem.stored, ENGINES)
    g.wait_ge(T.sem.stored, ENGINES)
